import numpy as np
import ml_dtypes


def mxq(x, axis, fmt="e4m3"):
    dtype, down = {"e4m3": (ml_dtypes.float8_e4m3fn, 7), "e5m2": (ml_dtypes.float8_e5m2, 14)}[fmt]
    v = np.moveaxis(np.asarray(x, np.float32).astype(ml_dtypes.bfloat16).astype(np.float64), axis, -1)
    blocks = v.reshape(v.shape[:-1] + (-1, 32))
    amax = np.abs(blocks).max(-1, keepdims=True)
    byte = np.maximum(np.where(amax > 0, np.frexp(amax)[1] - 1 + 127, 0) - down, 1)
    scale = np.exp2(byte - 127.0)
    codes = (blocks / scale).astype(np.float32).astype(dtype).astype(np.float64)
    return np.moveaxis((codes * scale).reshape(v.shape), -1, axis)


WIDE = False


def mx_kscale(k):
    if not WIDE:
        return np.ones(k)
    levels = np.array([30, -30])
    if k % 512:
        return np.exp2(np.random.permutation(np.resize(levels, k // 32))).repeat(32)
    a = np.empty((k // 512, 16))
    for p in range(k // 512):
        a[p, :8] = np.random.permutation(np.resize(levels, 8))
        for g in range(8):
            far = levels[np.abs(levels - a[p, g]) >= 10]
            a[p, g + 8] = far[np.random.randint(len(far))]
    return np.exp2(a.ravel()).repeat(32)


def f64(x):
    return np.asarray(x).astype(np.float64)


E2M1 = np.array([0.0, 0.5, 1.0, 1.5, 2.0, 3.0, 4.0, 6.0, -0.0, -0.5, -1.0, -1.5, -2.0, -3.0, -4.0, -6.0])


def pack_weight(w, fmt):
    k, n = w.shape
    w = f64(np.asarray(w, np.float32).astype(ml_dtypes.bfloat16)).reshape(k // 32, 32, n)
    amax = np.abs(w).max(1)
    if fmt == "e4m3":
        byte = np.frexp(amax)[1] - 1 + 127 - 7
    else:
        mant, ex = np.frexp(amax / 6.0)
        byte = np.where(mant > 0.5, ex, ex - 1) + 127
    byte = np.clip(np.where(amax > 0, byte, 1), 1, 254)
    scaled = (w * np.exp2(127.0 - byte)[:, None, :]).reshape(k, n).astype(np.float32)
    by_word = np.ascontiguousarray(scaled.reshape(k // 512, 128, 4, n).transpose(0, 1, 3, 2))
    if fmt == "e4m3":
        words = by_word.astype(ml_dtypes.float8_e4m3fn).view(np.uint8)
    else:
        c = by_word.astype(ml_dtypes.float4_e2m1fn).view(np.uint8) & 0xF
        words = (c[..., 0::2] | (c[..., 1::2] << 4)).reshape(k // 512, 128, 2 * n)
    return np.ascontiguousarray(words), np.ascontiguousarray(byte.astype(np.uint8).reshape(k // 512, 16, n))


def unpack_weight(words, scales, fmt):
    g, _, n = scales.shape
    words = np.ascontiguousarray(words).reshape(g, 128, n, -1)
    if fmt == "e4m3":
        vals = words.view(ml_dtypes.float8_e4m3fn).astype(np.float64)
    else:
        nib = np.empty((g, 128, n, 4), np.uint8)
        nib[..., 0::2] = words & 0xF
        nib[..., 1::2] = words >> 4
        vals = E2M1[nib]
    vals = vals * np.repeat(np.exp2(scales.astype(np.float64) - 127.0), 8, axis=1)[..., None]
    return vals.transpose(0, 1, 3, 2).reshape(g * 512, n)


N, L, R, K, T, B = 512, 1024, 512, 512, 512, 128


def setup_inputs():
    n = np.random.standard_normal
    fn = mx_kscale(N)
    fl = mx_kscale(L)
    fr = mx_kscale(R)
    wdp = pack_weight(n((N, R)) * 1 / np.sqrt(N) * fn[:, None], "e2m1")
    xqp = pack_weight(n((L, T)) / fl[:, None], "e4m3")
    wsp = pack_weight(n((L, R)) * 1 / np.sqrt(L) * fl[:, None], "e2m1")
    wup = pack_weight(n((R, K)) * 1 / np.sqrt(R) / fr[:, None], "e4m3")
    return {
        "g": (n((N, T)) * np.exp(0.5 * n((1, T))) / fn[:, None]).astype(np.float32),
        "wd_words": wdp[0],
        "wd_scales": wdp[1],
        "xq_words": xqp[0],
        "xq_scales": xqp[1],
        "ws_words": wsp[0],
        "ws_scales": wsp[1],
        "us": (np.random.uniform(0.5, 2.0, (R, 1)) * fr[:, None]).astype(np.float32),
        "wu_words": wup[0],
        "wu_scales": wup[1],
    }


def reference(g, wd_words, wd_scales, xq_words, xq_scales, ws_words, ws_scales, us, wu_words, wu_scales):
    wdu = unpack_weight(wd_words, wd_scales, "e2m1")
    xqu = unpack_weight(xq_words, xq_scales, "e4m3")
    wsu = unpack_weight(ws_words, ws_scales, "e2m1")
    wuu = unpack_weight(wu_words, wu_scales, "e4m3")
    gq = mxq(f64(g), 0, "e5m2")
    d = wdu.T @ gq + wsu.T @ xqu
    m = d.reshape(R, B, T // B).mean(axis=2)
    mr = np.repeat(m, T // B, axis=1)
    dz = (0.5 * d + 0.5 * mr) * f64(us)
    dzq = mxq(dz, 0, "e5m2")
    y = wuu.T @ dzq
    return y

@@ -1,0 +1,250 @@
+from contextlib import ExitStack
+
+import concourse.mybir as mybir
+
+N, L, R, K, T = 512, 1024, 512, 512, 512
+FLOPS = 2 * R * T * (N + L) + 2 * K * T * R
+
+F32 = mybir.dt.float32
+BF16 = mybir.dt.bfloat16
+I32 = mybir.dt.int32
+U32 = mybir.dt.uint32
+U16 = mybir.dt.uint16
+U8 = mybir.dt.uint8
+E4M3 = mybir.dt.float8_e4m3fn_x4
+E5M2 = mybir.dt.float8_e5m2_x4
+E2M1 = mybir.dt.float4_e2m1fn_x4
+ALU = mybir.AluOpType
+ACT = mybir.ActivationFunctionType
+AXIS = mybir.AxisListType
+
+P = 128
+PACK = 4
+GROUP = 4
+HALF = T // 2
+G_DVE_COLS = 192
+
+
+def load_scales(queue, plane, scales):
+    rows = scales.bitcast(I32)
+    for q in range(4):
+        queue.dma_start(
+            out=plane[32 * q : 32 * q + 4, :, :].bitcast(I32),
+            in_=rows[:, 4 * q : 4 * q + 4, :].rearrange("z r c -> r z c"),
+        )
+
+
+def regroup_words(nc, dst, src):
+    nc.vector.tensor_copy(
+        out=dst.bitcast(U16).rearrange("p (j a m) -> p a j m", j=PACK, m=8),
+        in_=src.bitcast(U16).rearrange("p (a m j) -> p a j m", j=PACK, m=8),
+    )
+
+
+def regroup_scales(nc, dst, src):
+    nc.vector.tensor_copy(
+        out=dst.rearrange("p (j a m) -> p a j m", j=PACK, m=16),
+        in_=src.rearrange("p (a m j) -> p a j m", j=PACK, m=16),
+    )
+
+
+def cast_views(dst, src):
+    return (
+        dst.rearrange("p (c i) j -> p c j i", i=4),
+        src.rearrange("p j (c i) -> p c j i", i=4),
+    )
+
+
+def tile_mix_gradient_shared_by_neighbours_kernel(
+    tc, g, wd_words, wd_scales, xq_words, xq_scales, ws_words, ws_scales, us, wu_words, wu_scales, out
+):
+    nc = tc.nc
+    with ExitStack() as ctx:
+        sb = ctx.enter_context(tc.tile_pool(name="sb", bufs=1))
+        psum = ctx.enter_context(tc.psum_pool(name="psum", bufs=1))
+        ctx.enter_context(tc.manual_schedule())
+
+        def tile(name, shape, dtype):
+            return sb.tile(shape, dtype, name=name, align_bytes=64)
+
+        ws_raw = tile("ws_raw", [P, 2, 2 * R], U8)
+        staged = tile("staged", [16, 5 * R // 4], I32)
+        planes = tile("planes", [P, 5 * R], U8)
+        wd_raw = tile("wd_raw", [P, 1, 2 * R], U8)
+        w_codes = [tile("w_codes%d" % z, [P, 2 * R], U8) for z in range(3)]
+        w_plane = [tile("w_plane%d" % z, [P, R], U8) for z in range(3)]
+        xq_codes = tile("xq_codes", [P, 2, T], I32)
+        wu_codes = tile("wu_codes", [P, K], I32)
+        wu_plane = tile("wu_plane", [P, 1, K], U8)
+        g_raw = [tile("g_raw%d" % h, [P, PACK, HALF], F32) for h in range(2)]
+        g_bf = [tile("g_bf%d" % h, [P, HALF, PACK], BF16) for h in range(2)]
+        g_codes = tile("g_codes", [P, T], U32)
+        g_plane = tile("g_plane", [P, T], U8)
+        us_sb = tile("us_sb", [P, PACK], F32)
+        us_half = tile("us_half", [P, PACK], F32)
+        table = tile("table", [P, 8], F32)
+        own = tile("own", [P, PACK, T], F32)
+        sums = tile("sums", [P, PACK, T // GROUP], F32)
+        shared = tile("shared", [P, PACK, T // GROUP], F32)
+        dz_bf = [tile("dz_bf%d" % u, [P, T // 4, PACK], BF16) for u in range(4)]
+        dz_codes = tile("dz_codes", [P, 3 * HALF], U32)
+        dz_plane = tile("dz_plane", [P, 3 * HALF], U8)
+        res = [[tile("res%d_%d" % (h, c), [P, HALF], F32) for c in range(4)] for h in range(2)]
+        banks = [psum.tile([P, T], F32, name="bank%d" % b) for b in range(8)]
+
+        nc.vector.memset(planes[:].bitcast(I32), 0)
+        nc.gpsimd.memset(table[:], 0.0)
+        nc.gpsimd.memset(wu_plane[:].bitcast(I32), 0)
+        nc.gpsimd.memset(dz_codes[:, HALF : 2 * HALF], 0)
+        nc.gpsimd.memset(dz_plane[:, HALF : 2 * HALF].bitcast(I32), 0)
+
+        plane_words = planes[:].bitcast(I32)
+        row = R // 4
+        for first, scales in ((0, ws_scales), (2, xq_scales), (4, wd_scales)):
+            passes = scales.shape[0]
+            nc.scalar.dma_start(
+                out=staged[:, first * row : (first + passes) * row].rearrange("q (z c) -> q z c", z=passes),
+                in_=scales.bitcast(I32).rearrange("z q c -> q z c"),
+            )
+        nc.sync.dma_start(out=ws_raw[:].bitcast(I32), in_=ws_words.bitcast(I32).rearrange("z p c -> p z c"))
+        nc.sync.dma_start(out=wd_raw[:].bitcast(I32), in_=wd_words.bitcast(I32).rearrange("z p c -> p z c"))
+        nc.sync.dma_start(out=xq_codes[:], in_=xq_words.rearrange("z p n t -> p z (n t)").bitcast(I32))
+        g_rows = g.rearrange("(p j) t -> p j t", j=PACK)
+        for h in range(2):
+            nc.sync.dma_start(out=g_raw[h][:], in_=g_rows[:, :, h * HALF : (h + 1) * HALF])
+        nc.scalar.activation(out=table[:, 4:5], in_=table[:, 0:1], func=ACT.Copy)
+        for q in range(4):
+            nc.scalar.dma_start(out=plane_words[32 * q : 32 * q + 4, :], in_=staged[4 * q : 4 * q + 4, :])
+        nc.sync.dma_start(out=us_sb[:], in_=us.rearrange("(p j) o -> p (j o)", j=PACK))
+        nc.sync.dma_start(out=wu_codes[:], in_=wu_words[0].rearrange("p n t -> p (n t)").bitcast(I32))
+        load_scales(nc.sync, wu_plane, wu_scales)
+
+        regroup_words(nc, w_codes[0][:], ws_raw[:, 0, :])
+        regroup_words(nc, w_codes[1][:], ws_raw[:, 1, :])
+        regroup_words(nc, w_codes[2][:], wd_raw[:, 0, :])
+        for z, first in enumerate((0, 1, 4)):
+            regroup_scales(nc, w_plane[z][:], planes[:, first * R : (first + 1) * R])
+
+        dst, src = cast_views(g_bf[0][:], g_raw[0][:])
+        nc.scalar.copy(out=dst, in_=src)
+        dst, src = cast_views(g_bf[1][:, :G_DVE_COLS, :], g_raw[1][:, :, :G_DVE_COLS])
+        nc.vector.tensor_copy(out=dst, in_=src)
+        dst, src = cast_views(g_bf[1][:, G_DVE_COLS:, :], g_raw[1][:, :, G_DVE_COLS:])
+        nc.scalar.copy(out=dst, in_=src)
+        nc.scalar.activation(out=us_half[:], in_=us_sb[:], func=ACT.Copy, scale=0.5)
+        for h in range(2):
+            cols = slice(h * HALF, (h + 1) * HALF)
+            nc.vector.quantize_mx(
+                out=g_codes[:, cols].bitcast(E5M2),
+                scales=g_plane[:, cols],
+                in_=g_bf[h][:].rearrange("p t j -> p (t j)"),
+            )
+
+        moving = [
+            (xq_codes[:, 0, :].bitcast(E4M3), planes[:, 2 * R : 3 * R]),
+            (xq_codes[:, 1, :].bitcast(E4M3), planes[:, 3 * R : 4 * R]),
+            (g_codes[:].bitcast(E5M2), g_plane[:]),
+        ]
+        for z in range(3):
+            for j in range(PACK):
+                nc.tensor.matmul_mx(
+                    out=banks[j][:],
+                    lhsT=w_codes[z][:, 2 * P * j : 2 * P * (j + 1)].bitcast(E2M1),
+                    lhsT_scale=w_plane[z][:, P * j : P * (j + 1)],
+                    rhs=moving[z][0],
+                    rhs_scale=moving[z][1],
+                    start=(z == 0),
+                    stop=(z == 2),
+                )
+
+        def group_sum(j):
+            nc.vector.tensor_reduce(
+                out=sums[:, j, :],
+                in_=banks[j][:].rearrange("p (b i) -> p b i", i=GROUP),
+                axis=AXIS.X,
+                op=ALU.add,
+            )
+
+        def own_part(j):
+            nc.scalar.activation(out=own[:, j, :], in_=banks[j][:], func=ACT.Copy, scale=us_half[:, j : j + 1])
+
+        def shared_part(engine, j):
+            engine.tensor_scalar(
+                out=shared[:, j, :],
+                in0=sums[:, j, :],
+                scalar1=us_half[:, j : j + 1],
+                scalar2=1.0 / GROUP,
+                op0=ALU.mult,
+                op1=ALU.mult,
+            )
+
+        for js, jo in ((0, 1), (2, 0), (3, 2), (1, 3)):
+            group_sum(js)
+            own_part(jo)
+            shared_part(nc.vector if js == 1 else nc.gpsimd, js)
+
+        for j, passes in ((0, 2), (2, 2), (3, 3)):
+            for rep in range(passes):
+                nc.tensor.matmul_mx(
+                    out=banks[j][:],
+                    lhsT=w_codes[2][:, : 2 * P].bitcast(E2M1),
+                    lhsT_scale=w_plane[2][:, :P],
+                    rhs=moving[2][0],
+                    rhs_scale=moving[2][1],
+                    start=True,
+                    stop=True,
+                )
+
+        quarter = T // 4
+        groups = quarter // GROUP
+
+        def blend(u):
+            nc.vector.tensor_tensor(
+                out=dz_bf[u][:].rearrange("p (b i) j -> p b j i", i=GROUP),
+                in0=own[:, :, u * quarter : (u + 1) * quarter].rearrange("p j (b i) -> p b j i", i=GROUP),
+                in1=shared[:, :, u * groups : (u + 1) * groups]
+                .rearrange("p j b -> p b j")
+                .unsqueeze(3)
+                .to_broadcast([P, groups, PACK, GROUP]),
+                op=ALU.add,
+            )
+
+        def quantize(u):
+            first = u * quarter + (u // 2) * HALF
+            cols = slice(first, first + quarter)
+            nc.vector.quantize_mx(
+                out=dz_codes[:, cols].bitcast(E5M2),
+                scales=dz_plane[:, cols],
+                in_=dz_bf[u][:].rearrange("p t j -> p (t j)"),
+            )
+
+        def second_layer(h):
+            window = slice(h * HALF, h * HALF + T)
+            tokens = slice(h * HALF, (h + 1) * HALF)
+            for c in range(4):
+                bank = banks[4 * (1 - h) + c]
+                nc.tensor.matmul_mx(
+                    out=bank[:],
+                    lhsT=wu_codes[:, P * c : P * (c + 1)].bitcast(E4M3),
+                    lhsT_scale=wu_plane[:, 0, P * c : P * (c + 1)],
+                    rhs=dz_codes[:, window].bitcast(E5M2),
+                    rhs_scale=dz_plane[:, window],
+                    start=True,
+                    stop=True,
+                )
+                if h == 1 and c % 2 == 1:
+                    nc.vector.tensor_copy(out=res[h][c][:], in_=bank[:, tokens])
+                else:
+                    nc.scalar.copy(out=res[h][c][:], in_=bank[:, tokens])
+                nc.sync.dma_start(out=out[P * c : P * (c + 1), tokens], in_=res[h][c][:])
+
+        blend(0)
+        blend(1)
+        quantize(0)
+        blend(2)
+        quantize(1)
+        second_layer(0)
+        blend(3)
+        quantize(2)
+        quantize(3)
+        second_layer(1)

@@ -22,7 +22,9 @@ P = 128
 PACK = 4
 GROUP = 4
 HALF = T // 2
-G_DVE_COLS = 192
+QUARTER = T // 4
+G_DVE_COLS = 96
+WARM_UP = 3
 
 
 def load_scales(queue, plane, scales):
@@ -68,163 +70,183 @@ def tile_mix_gradient_shared_by_neighbours_kernel(
             return sb.tile(shape, dtype, name=name, align_bytes=64)
 
         ws_raw = tile("ws_raw", [P, 2, 2 * R], U8)
-        staged = tile("staged", [16, 5 * R // 4], I32)
+        wd_raw = tile("wd_raw", [P, 2 * R], U8)
+        staged = tile("staged", [P, 5 * R], U8)
         planes = tile("planes", [P, 5 * R], U8)
-        wd_raw = tile("wd_raw", [P, 1, 2 * R], U8)
         w_codes = [tile("w_codes%d" % z, [P, 2 * R], U8) for z in range(3)]
         w_plane = [tile("w_plane%d" % z, [P, R], U8) for z in range(3)]
-        xq_codes = tile("xq_codes", [P, 2, T], I32)
+        xq_codes = [tile("xq_codes%d" % h, [P, 2 * HALF], I32) for h in range(2)]
         wu_codes = tile("wu_codes", [P, K], I32)
         wu_plane = tile("wu_plane", [P, 1, K], U8)
         g_raw = [tile("g_raw%d" % h, [P, PACK, HALF], F32) for h in range(2)]
         g_bf = [tile("g_bf%d" % h, [P, HALF, PACK], BF16) for h in range(2)]
-        g_codes = tile("g_codes", [P, T], U32)
-        g_plane = tile("g_plane", [P, T], U8)
+        g_codes = tile("g_codes", [P, 3 * HALF], U32)
+        g_plane = tile("g_plane", [P, 3 * HALF], U8)
         us_sb = tile("us_sb", [P, PACK], F32)
         us_half = tile("us_half", [P, PACK], F32)
+        us_eighth = tile("us_eighth", [P, PACK], F32)
         table = tile("table", [P, 8], F32)
-        own = tile("own", [P, PACK, T], F32)
-        sums = tile("sums", [P, PACK, T // GROUP], F32)
-        shared = tile("shared", [P, PACK, T // GROUP], F32)
-        dz_bf = [tile("dz_bf%d" % u, [P, T // 4, PACK], BF16) for u in range(4)]
+        own = [tile("own%d" % h, [P, PACK, HALF], F32) for h in range(2)]
+        sums = [tile("sums%d" % h, [P, PACK, HALF // GROUP], F32) for h in range(2)]
+        shared = [tile("shared%d" % h, [P, PACK, HALF // GROUP], F32) for h in range(2)]
+        dz_bf = [tile("dz_bf%d" % u, [P, QUARTER, PACK], BF16) for u in range(4)]
         dz_codes = tile("dz_codes", [P, 3 * HALF], U32)
         dz_plane = tile("dz_plane", [P, 3 * HALF], U8)
         res = [[tile("res%d_%d" % (h, c), [P, HALF], F32) for c in range(4)] for h in range(2)]
-        banks = [psum.tile([P, T], F32, name="bank%d" % b) for b in range(8)]
+        banks = [[psum.tile([P, T], F32, name="bank%d_%d" % (h, j)) for j in range(PACK)] for h in range(2)]
 
+        filler = slice(HALF, 2 * HALF)
+        nc.gpsimd.memset(staged[:, 2 * R : 3 * R].bitcast(I32), 0)
         nc.vector.memset(planes[:].bitcast(I32), 0)
         nc.gpsimd.memset(table[:], 0.0)
+        nc.gpsimd.memset(g_plane[:, filler].bitcast(I32), 0)
+        nc.gpsimd.memset(g_codes[:, filler], 0)
+        nc.gpsimd.memset(dz_plane[:, filler].bitcast(I32), 0)
+        nc.gpsimd.memset(dz_codes[:, filler], 0)
         nc.gpsimd.memset(wu_plane[:].bitcast(I32), 0)
-        nc.gpsimd.memset(dz_codes[:, HALF : 2 * HALF], 0)
-        nc.gpsimd.memset(dz_plane[:, HALF : 2 * HALF].bitcast(I32), 0)
 
+        staged_words = staged[:].bitcast(I32)
         plane_words = planes[:].bitcast(I32)
         row = R // 4
-        for first, scales in ((0, ws_scales), (2, xq_scales), (4, wd_scales)):
+        for first, scales in ((0, ws_scales), (4, wd_scales), (2, xq_scales)):
             passes = scales.shape[0]
-            nc.scalar.dma_start(
-                out=staged[:, first * row : (first + passes) * row].rearrange("q (z c) -> q z c", z=passes),
+            nc.sync.dma_start(
+                out=staged_words[0:16, first * row : (first + passes) * row].rearrange("q (z c) -> q z c", z=passes),
                 in_=scales.bitcast(I32).rearrange("z q c -> q z c"),
             )
-        nc.sync.dma_start(out=ws_raw[:].bitcast(I32), in_=ws_words.bitcast(I32).rearrange("z p c -> p z c"))
-        nc.sync.dma_start(out=wd_raw[:].bitcast(I32), in_=wd_words.bitcast(I32).rearrange("z p c -> p z c"))
-        nc.sync.dma_start(out=xq_codes[:], in_=xq_words.rearrange("z p n t -> p z (n t)").bitcast(I32))
         g_rows = g.rearrange("(p j) t -> p j t", j=PACK)
-        for h in range(2):
-            nc.sync.dma_start(out=g_raw[h][:], in_=g_rows[:, :, h * HALF : (h + 1) * HALF])
-        nc.scalar.activation(out=table[:, 4:5], in_=table[:, 0:1], func=ACT.Copy)
+        xq_rows = xq_words.rearrange("z p n t -> p z (n t)").bitcast(I32)
+
+        def load_xq(h):
+            nc.sync.dma_start(
+                out=xq_codes[h][:].rearrange("p (z t) -> p z t", z=2), in_=xq_rows[:, :, h * HALF : (h + 1) * HALF]
+            )
+
+        nc.sync.dma_start(out=wd_raw[:].bitcast(I32), in_=wd_words[0].bitcast(I32))
+        load_xq(0)
+        nc.sync.dma_start(out=g_raw[0][:], in_=g_rows[:, :, :HALF])
+        nc.scalar.dma_start(out=us_sb[:], in_=us.rearrange("(p j) o -> p (j o)", j=PACK))
         for q in range(4):
-            nc.scalar.dma_start(out=plane_words[32 * q : 32 * q + 4, :], in_=staged[4 * q : 4 * q + 4, :])
-        nc.sync.dma_start(out=us_sb[:], in_=us.rearrange("(p j) o -> p (j o)", j=PACK))
+            nc.sync.dma_start(out=plane_words[32 * q : 32 * q + 4, :], in_=staged_words[4 * q : 4 * q + 4, :])
+        nc.sync.dma_start(out=ws_raw[:].bitcast(I32), in_=ws_words.bitcast(I32).rearrange("z p c -> p z c"))
+        nc.sync.dma_start(out=g_raw[1][:], in_=g_rows[:, :, HALF:])
+        load_xq(1)
         nc.sync.dma_start(out=wu_codes[:], in_=wu_words[0].rearrange("p n t -> p (n t)").bitcast(I32))
         load_scales(nc.sync, wu_plane, wu_scales)
 
-        regroup_words(nc, w_codes[0][:], ws_raw[:, 0, :])
-        regroup_words(nc, w_codes[1][:], ws_raw[:, 1, :])
-        regroup_words(nc, w_codes[2][:], wd_raw[:, 0, :])
-        for z, first in enumerate((0, 1, 4)):
-            regroup_scales(nc, w_plane[z][:], planes[:, first * R : (first + 1) * R])
-
-        dst, src = cast_views(g_bf[0][:], g_raw[0][:])
-        nc.scalar.copy(out=dst, in_=src)
-        dst, src = cast_views(g_bf[1][:, :G_DVE_COLS, :], g_raw[1][:, :, :G_DVE_COLS])
-        nc.vector.tensor_copy(out=dst, in_=src)
-        dst, src = cast_views(g_bf[1][:, G_DVE_COLS:, :], g_raw[1][:, :, G_DVE_COLS:])
-        nc.scalar.copy(out=dst, in_=src)
+        nc.scalar.activation(out=table[:, 4:5], in_=table[:, 0:1], func=ACT.Copy)
         nc.scalar.activation(out=us_half[:], in_=us_sb[:], func=ACT.Copy, scale=0.5)
-        for h in range(2):
-            cols = slice(h * HALF, (h + 1) * HALF)
+        nc.scalar.activation(out=us_eighth[:], in_=us_sb[:], func=ACT.Copy, scale=0.5 / GROUP)
+
+        for rep in range(WARM_UP):
+            nc.tensor.matmul_mx(
+                out=banks[1][3][:],
+                lhsT=wd_raw[:, : 2 * P].bitcast(E2M1),
+                lhsT_scale=staged[:, 2 * R : 2 * R + P],
+                rhs=xq_codes[0][:].bitcast(E4M3),
+                rhs_scale=staged[:, 2 * R : 3 * R],
+                start=True,
+                stop=True,
+            )
+
+        def cast_g(copy, h, cols):
+            dst, src = cast_views(g_bf[h][:, cols, :], g_raw[h][:, :, cols])
+            copy(out=dst, in_=src)
+
+        def quantize_g(h):
+            cols = slice(2 * h * HALF, (2 * h + 1) * HALF)
             nc.vector.quantize_mx(
                 out=g_codes[:, cols].bitcast(E5M2),
                 scales=g_plane[:, cols],
                 in_=g_bf[h][:].rearrange("p t j -> p (t j)"),
             )
 
-        moving = [
-            (xq_codes[:, 0, :].bitcast(E4M3), planes[:, 2 * R : 3 * R]),
-            (xq_codes[:, 1, :].bitcast(E4M3), planes[:, 3 * R : 4 * R]),
-            (g_codes[:].bitcast(E5M2), g_plane[:]),
-        ]
-        for z in range(3):
-            for j in range(PACK):
-                nc.tensor.matmul_mx(
-                    out=banks[j][:],
-                    lhsT=w_codes[z][:, 2 * P * j : 2 * P * (j + 1)].bitcast(E2M1),
-                    lhsT_scale=w_plane[z][:, P * j : P * (j + 1)],
-                    rhs=moving[z][0],
-                    rhs_scale=moving[z][1],
-                    start=(z == 0),
-                    stop=(z == 2),
-                )
+        def first_sum_pass(h, j, z, cols, codes, plane, start, stop):
+            nc.tensor.matmul_mx(
+                out=banks[h][j][:, cols],
+                lhsT=w_codes[z][:, 2 * P * j : 2 * P * (j + 1)].bitcast(E2M1),
+                lhsT_scale=w_plane[z][:, P * j : P * (j + 1)],
+                rhs=codes,
+                rhs_scale=plane,
+                start=start,
+                stop=stop,
+            )
 
-        def group_sum(j):
+        def first_sum(h):
+            window = slice(h * HALF, h * HALF + T)
+            for j in range(PACK):
+                first_sum_pass(
+                    h, j, 2, slice(0, T), g_codes[:, window].bitcast(E5M2), g_plane[:, window], True, False
+                )
+            for j in range(PACK):
+                for z in range(2):
+                    for part in range(2):
+                        first = h * HALF + part * QUARTER
+                        at = z * HALF + part * QUARTER
+                        first_sum_pass(
+                            h,
+                            j,
+                            z,
+                            slice(first, first + QUARTER),
+                            xq_codes[h][:, at : at + QUARTER].bitcast(E4M3),
+                            planes[:, (2 + z) * R + first : (2 + z) * R + first + QUARTER],
+                            False,
+                            z == 1 and part == 1,
+                        )
+
+        def group_sums(h, j):
             nc.vector.tensor_reduce(
-                out=sums[:, j, :],
-                in_=banks[j][:].rearrange("p (b i) -> p b i", i=GROUP),
+                out=sums[h][:, j, :],
+                in_=banks[h][j][:, h * HALF : (h + 1) * HALF].rearrange("p (b i) -> p b i", i=GROUP),
                 axis=AXIS.X,
                 op=ALU.add,
             )
 
-        def own_part(j):
-            nc.scalar.activation(out=own[:, j, :], in_=banks[j][:], func=ACT.Copy, scale=us_half[:, j : j + 1])
-
-        def shared_part(engine, j):
-            engine.tensor_scalar(
-                out=shared[:, j, :],
-                in0=sums[:, j, :],
-                scalar1=us_half[:, j : j + 1],
-                scalar2=1.0 / GROUP,
-                op0=ALU.mult,
-                op1=ALU.mult,
+        def own_part(h, j):
+            nc.scalar.activation(
+                out=own[h][:, j, :],
+                in_=banks[h][j][:, h * HALF : (h + 1) * HALF],
+                func=ACT.Copy,
+                scale=us_half[:, j : j + 1],
             )
 
-        for js, jo in ((0, 1), (2, 0), (3, 2), (1, 3)):
-            group_sum(js)
-            own_part(jo)
-            shared_part(nc.vector if js == 1 else nc.gpsimd, js)
-
-        for j, passes in ((0, 2), (2, 2), (3, 3)):
-            for rep in range(passes):
-                nc.tensor.matmul_mx(
-                    out=banks[j][:],
-                    lhsT=w_codes[2][:, : 2 * P].bitcast(E2M1),
-                    lhsT_scale=w_plane[2][:, :P],
-                    rhs=moving[2][0],
-                    rhs_scale=moving[2][1],
-                    start=True,
-                    stop=True,
-                )
-
-        quarter = T // 4
-        groups = quarter // GROUP
+        def shared_part(engine, h, j):
+            engine.tensor_scalar(
+                out=shared[h][:, j, :],
+                in0=sums[h][:, j, :],
+                scalar1=us_eighth[:, j : j + 1],
+                scalar2=0.0,
+                op0=ALU.mult,
+                op1=ALU.add,
+            )
 
         def blend(u):
+            h, part = divmod(u, 2)
+            groups = QUARTER // GROUP
             nc.vector.tensor_tensor(
                 out=dz_bf[u][:].rearrange("p (b i) j -> p b j i", i=GROUP),
-                in0=own[:, :, u * quarter : (u + 1) * quarter].rearrange("p j (b i) -> p b j i", i=GROUP),
-                in1=shared[:, :, u * groups : (u + 1) * groups]
+                in0=own[h][:, :, part * QUARTER : (part + 1) * QUARTER].rearrange("p j (b i) -> p b j i", i=GROUP),
+                in1=shared[h][:, :, part * groups : (part + 1) * groups]
                 .rearrange("p j b -> p b j")
                 .unsqueeze(3)
                 .to_broadcast([P, groups, PACK, GROUP]),
                 op=ALU.add,
             )
 
-        def quantize(u):
-            first = u * quarter + (u // 2) * HALF
-            cols = slice(first, first + quarter)
+        def quantize_dz(u):
+            first = u * QUARTER + (u // 2) * HALF
+            cols = slice(first, first + QUARTER)
             nc.vector.quantize_mx(
                 out=dz_codes[:, cols].bitcast(E5M2),
                 scales=dz_plane[:, cols],
                 in_=dz_bf[u][:].rearrange("p t j -> p (t j)"),
             )
 
-        def second_layer(h):
+        def first_layer(h):
             window = slice(h * HALF, h * HALF + T)
-            tokens = slice(h * HALF, (h + 1) * HALF)
             for c in range(4):
-                bank = banks[4 * (1 - h) + c]
                 nc.tensor.matmul_mx(
-                    out=bank[:],
+                    out=banks[h][c][:],
                     lhsT=wu_codes[:, P * c : P * (c + 1)].bitcast(E4M3),
                     lhsT_scale=wu_plane[:, 0, P * c : P * (c + 1)],
                     rhs=dz_codes[:, window].bitcast(E5M2),
@@ -232,19 +254,61 @@ def tile_mix_gradient_shared_by_neighbours_kernel(
                     start=True,
                     stop=True,
                 )
+
+        def store(h):
+            tokens = slice(h * HALF, (h + 1) * HALF)
+            for c in range(4):
                 if h == 1 and c % 2 == 1:
-                    nc.vector.tensor_copy(out=res[h][c][:], in_=bank[:, tokens])
+                    nc.vector.tensor_copy(out=res[h][c][:], in_=banks[h][c][:, tokens])
                 else:
-                    nc.scalar.copy(out=res[h][c][:], in_=bank[:, tokens])
+                    nc.scalar.copy(out=res[h][c][:], in_=banks[h][c][:, tokens])
                 nc.sync.dma_start(out=out[P * c : P * (c + 1), tokens], in_=res[h][c][:])
 
+        def cast_half(h):
+            cast_g(nc.vector.tensor_copy, h, slice(0, G_DVE_COLS))
+            cast_g(nc.scalar.copy, h, slice(G_DVE_COLS, HALF))
+
+        regroup_words(nc, w_codes[2][:], wd_raw[:])
+        cast_half(0)
+        regroup_scales(nc, w_plane[2][:], planes[:, 4 * R : 5 * R])
+        quantize_g(0)
+        for z in range(2):
+            regroup_scales(nc, w_plane[z][:], planes[:, z * R : (z + 1) * R])
+        for z in range(2):
+            regroup_words(nc, w_codes[z][:], ws_raw[:, z, :])
+        first_sum(0)
+        cast_half(1)
+        quantize_g(1)
+        first_sum(1)
+        for js, jo in ((0, 1), (2, 0), (3, 2), (1, 3)):
+            group_sums(0, js)
+            own_part(0, jo)
+            shared_part(nc.vector if js == 1 else nc.gpsimd, 0, js)
+        for j in range(PACK):
+            own_part(1, j)
         blend(0)
         blend(1)
-        quantize(0)
+        quantize_dz(0)
+        for j in range(PACK):
+            group_sums(1, j)
+            if j == 0:
+                quantize_dz(1)
+            shared_part(nc.vector if j == PACK - 1 else nc.gpsimd, 1, j)
+        first_layer(0)
+        store(0)
+        for c in (2, 3, 3):
+            nc.tensor.matmul_mx(
+                out=banks[0][c][:],
+                lhsT=wu_codes[:, :P].bitcast(E4M3),
+                lhsT_scale=wu_plane[:, 0, :P],
+                rhs=dz_codes[:, :T].bitcast(E5M2),
+                rhs_scale=dz_plane[:, :T],
+                start=True,
+                stop=True,
+            )
         blend(2)
-        quantize(1)
-        second_layer(0)
         blend(3)
-        quantize(2)
-        quantize(3)
-        second_layer(1)
+        quantize_dz(2)
+        quantize_dz(3)
+        first_layer(1)
+        store(1)

@@ -23,13 +23,14 @@ PACK = 4
 GROUP = 4
 HALF = T // 2
 QUARTER = T // 4
-G_DVE_COLS = 96
+G_DVE_COLS = 176
+G_DVE_COLS_2 = 144
 WARM_UP = 3
 
 
-def load_scales(queue, plane, scales):
+def load_scales(queues, plane, scales):
     rows = scales.bitcast(I32)
-    for q in range(4):
+    for q, queue in enumerate(queues):
         queue.dma_start(
             out=plane[32 * q : 32 * q + 4, :, :].bitcast(I32),
             in_=rows[:, 4 * q : 4 * q + 4, :].rearrange("z r c -> r z c"),
@@ -69,12 +70,15 @@ def tile_mix_gradient_shared_by_neighbours_kernel(
         def tile(name, shape, dtype):
             return sb.tile(shape, dtype, name=name, align_bytes=64)
 
-        ws_raw = tile("ws_raw", [P, 2, 2 * R], U8)
+        ws_raw = tile("ws_raw", [P, 4 * R], U8)
         wd_raw = tile("wd_raw", [P, 2 * R], U8)
-        staged = tile("staged", [P, 5 * R], U8)
-        planes = tile("planes", [P, 5 * R], U8)
-        w_codes = [tile("w_codes%d" % z, [P, 2 * R], U8) for z in range(3)]
-        w_plane = [tile("w_plane%d" % z, [P, R], U8) for z in range(3)]
+        staged = tile("staged", [P, 4 * R], U8)
+        planes = tile("planes", [P, 4 * R], U8)
+        wd_plane_raw = tile("wd_plane_raw", [P, 1, R], U8)
+        ws_codes = tile("ws_codes", [P, 4 * R], U8)
+        ws_plane = tile("ws_plane", [P, 2 * R], U8)
+        wd_codes = tile("wd_codes", [P, 2 * R], U8)
+        wd_plane = tile("wd_plane", [P, R], U8)
         xq_codes = [tile("xq_codes%d" % h, [P, 2 * HALF], I32) for h in range(2)]
         wu_codes = tile("wu_codes", [P, K], I32)
         wu_plane = tile("wu_plane", [P, 1, K], U8)
@@ -96,24 +100,26 @@ def tile_mix_gradient_shared_by_neighbours_kernel(
         banks = [[psum.tile([P, T], F32, name="bank%d_%d" % (h, j)) for j in range(PACK)] for h in range(2)]
 
         filler = slice(HALF, 2 * HALF)
-        nc.gpsimd.memset(staged[:, 2 * R : 3 * R].bitcast(I32), 0)
+        nc.gpsimd.memset(wd_plane_raw[:].bitcast(I32), 0)
+        nc.vector.memset(staged[:, 2 * R : 3 * R].bitcast(I32), 0)
+        nc.vector.memset(table[:], 0.0)
         nc.vector.memset(planes[:].bitcast(I32), 0)
-        nc.gpsimd.memset(table[:], 0.0)
-        nc.gpsimd.memset(g_plane[:, filler].bitcast(I32), 0)
-        nc.gpsimd.memset(g_codes[:, filler], 0)
-        nc.gpsimd.memset(dz_plane[:, filler].bitcast(I32), 0)
-        nc.gpsimd.memset(dz_codes[:, filler], 0)
-        nc.gpsimd.memset(wu_plane[:].bitcast(I32), 0)
+        nc.vector.memset(g_plane[:, filler].bitcast(I32), 0)
+        nc.vector.memset(g_codes[:, filler], 0)
+        nc.vector.memset(dz_plane[:, filler].bitcast(I32), 0)
+        nc.vector.memset(dz_codes[:, filler], 0)
+        nc.vector.memset(wu_plane[:].bitcast(I32), 0)
 
         staged_words = staged[:].bitcast(I32)
         plane_words = planes[:].bitcast(I32)
         row = R // 4
-        for first, scales in ((0, ws_scales), (4, wd_scales), (2, xq_scales)):
-            passes = scales.shape[0]
+
+        def stage_scales(first, scales):
             nc.sync.dma_start(
-                out=staged_words[0:16, first * row : (first + passes) * row].rearrange("q (z c) -> q z c", z=passes),
+                out=staged_words[0:16, first * row : (first + 2) * row].rearrange("q (z c) -> q z c", z=2),
                 in_=scales.bitcast(I32).rearrange("z q c -> q z c"),
             )
+
         g_rows = g.rearrange("(p j) t -> p j t", j=PACK)
         xq_rows = xq_words.rearrange("z p n t -> p z (n t)").bitcast(I32)
 
@@ -122,21 +128,22 @@ def tile_mix_gradient_shared_by_neighbours_kernel(
                 out=xq_codes[h][:].rearrange("p (z t) -> p z t", z=2), in_=xq_rows[:, :, h * HALF : (h + 1) * HALF]
             )
 
+        stage_scales(0, ws_scales)
         nc.sync.dma_start(out=wd_raw[:].bitcast(I32), in_=wd_words[0].bitcast(I32))
+        stage_scales(2, xq_scales)
+        load_scales((nc.scalar, nc.scalar, nc.scalar, nc.gpsimd), wd_plane_raw, wd_scales)
+        nc.gpsimd.dma_start(out=us_sb[:], in_=us.rearrange("(p j) o -> p (j o)", j=PACK))
         load_xq(0)
         nc.sync.dma_start(out=g_raw[0][:], in_=g_rows[:, :, :HALF])
-        nc.scalar.dma_start(out=us_sb[:], in_=us.rearrange("(p j) o -> p (j o)", j=PACK))
         for q in range(4):
             nc.sync.dma_start(out=plane_words[32 * q : 32 * q + 4, :], in_=staged_words[4 * q : 4 * q + 4, :])
-        nc.sync.dma_start(out=ws_raw[:].bitcast(I32), in_=ws_words.bitcast(I32).rearrange("z p c -> p z c"))
+        nc.sync.dma_start(out=ws_raw[:].bitcast(I32).rearrange("p (z c) -> p z c", z=2), in_=ws_words.bitcast(I32).rearrange("z p c -> p z c"))
         nc.sync.dma_start(out=g_raw[1][:], in_=g_rows[:, :, HALF:])
         load_xq(1)
         nc.sync.dma_start(out=wu_codes[:], in_=wu_words[0].rearrange("p n t -> p (n t)").bitcast(I32))
-        load_scales(nc.sync, wu_plane, wu_scales)
+        load_scales((nc.sync,) * 4, wu_plane, wu_scales)
 
         nc.scalar.activation(out=table[:, 4:5], in_=table[:, 0:1], func=ACT.Copy)
-        nc.scalar.activation(out=us_half[:], in_=us_sb[:], func=ACT.Copy, scale=0.5)
-        nc.scalar.activation(out=us_eighth[:], in_=us_sb[:], func=ACT.Copy, scale=0.5 / GROUP)
 
         for rep in range(WARM_UP):
             nc.tensor.matmul_mx(
@@ -161,11 +168,11 @@ def tile_mix_gradient_shared_by_neighbours_kernel(
                 in_=g_bf[h][:].rearrange("p t j -> p (t j)"),
             )
 
-        def first_sum_pass(h, j, z, cols, codes, plane, start, stop):
+        def first_sum_pass(h, j, w_codes, w_plane, at, cols, codes, plane, start, stop):
             nc.tensor.matmul_mx(
                 out=banks[h][j][:, cols],
-                lhsT=w_codes[z][:, 2 * P * j : 2 * P * (j + 1)].bitcast(E2M1),
-                lhsT_scale=w_plane[z][:, P * j : P * (j + 1)],
+                lhsT=w_codes[:, 2 * P * at : 2 * P * (at + 1)].bitcast(E2M1),
+                lhsT_scale=w_plane[:, P * at : P * (at + 1)],
                 rhs=codes,
                 rhs_scale=plane,
                 start=start,
@@ -176,7 +183,7 @@ def tile_mix_gradient_shared_by_neighbours_kernel(
             window = slice(h * HALF, h * HALF + T)
             for j in range(PACK):
                 first_sum_pass(
-                    h, j, 2, slice(0, T), g_codes[:, window].bitcast(E5M2), g_plane[:, window], True, False
+                    h, j, wd_codes, wd_plane, j, slice(0, T), g_codes[:, window].bitcast(E5M2), g_plane[:, window], True, False
                 )
             for j in range(PACK):
                 for z in range(2):
@@ -186,7 +193,9 @@ def tile_mix_gradient_shared_by_neighbours_kernel(
                         first_sum_pass(
                             h,
                             j,
-                            z,
+                            ws_codes,
+                            ws_plane,
+                            2 * j + z,
                             slice(first, first + QUARTER),
                             xq_codes[h][:, at : at + QUARTER].bitcast(E4M3),
                             planes[:, (2 + z) * R + first : (2 + z) * R + first + QUARTER],
@@ -264,20 +273,18 @@ def tile_mix_gradient_shared_by_neighbours_kernel(
                     nc.scalar.copy(out=res[h][c][:], in_=banks[h][c][:, tokens])
                 nc.sync.dma_start(out=out[P * c : P * (c + 1), tokens], in_=res[h][c][:])
 
-        def cast_half(h):
-            cast_g(nc.vector.tensor_copy, h, slice(0, G_DVE_COLS))
-            cast_g(nc.scalar.copy, h, slice(G_DVE_COLS, HALF))
-
-        regroup_words(nc, w_codes[2][:], wd_raw[:])
-        cast_half(0)
-        regroup_scales(nc, w_plane[2][:], planes[:, 4 * R : 5 * R])
+        regroup_words(nc, wd_codes[:], wd_raw[:])
+        cast_g(nc.vector.tensor_copy, 0, slice(0, G_DVE_COLS))
+        cast_g(nc.scalar.copy, 0, slice(G_DVE_COLS, HALF))
+        nc.scalar.activation(out=us_half[:], in_=us_sb[:], func=ACT.Copy, scale=0.5)
+        nc.scalar.activation(out=us_eighth[:], in_=us_sb[:], func=ACT.Copy, scale=0.5 / GROUP)
+        regroup_scales(nc, wd_plane[:], wd_plane_raw[:, 0, :])
         quantize_g(0)
-        for z in range(2):
-            regroup_scales(nc, w_plane[z][:], planes[:, z * R : (z + 1) * R])
-        for z in range(2):
-            regroup_words(nc, w_codes[z][:], ws_raw[:, z, :])
+        regroup_scales(nc, ws_plane[:], planes[:, : 2 * R])
+        regroup_words(nc, ws_codes[:], ws_raw[:])
         first_sum(0)
-        cast_half(1)
+        cast_g(nc.vector.tensor_copy, 1, slice(0, G_DVE_COLS_2))
+        cast_g(nc.scalar.copy, 1, slice(G_DVE_COLS_2, HALF))
         quantize_g(1)
         first_sum(1)
         for js, jo in ((0, 1), (2, 0), (3, 2), (1, 3)):

@@ -25,7 +25,6 @@ HALF = T // 2
 QUARTER = T // 4
 G_DVE_COLS = 176
 G_DVE_COLS_2 = 144
-WARM_UP = 3
 
 
 def load_scales(queues, plane, scales):
@@ -89,7 +88,6 @@ def tile_mix_gradient_shared_by_neighbours_kernel(
         us_sb = tile("us_sb", [P, PACK], F32)
         us_half = tile("us_half", [P, PACK], F32)
         us_eighth = tile("us_eighth", [P, PACK], F32)
-        table = tile("table", [P, 8], F32)
         own = [tile("own%d" % h, [P, PACK, HALF], F32) for h in range(2)]
         sums = [tile("sums%d" % h, [P, PACK, HALF // GROUP], F32) for h in range(2)]
         shared = [tile("shared%d" % h, [P, PACK, HALF // GROUP], F32) for h in range(2)]
@@ -101,8 +99,6 @@ def tile_mix_gradient_shared_by_neighbours_kernel(
 
         filler = slice(HALF, 2 * HALF)
         nc.gpsimd.memset(wd_plane_raw[:].bitcast(I32), 0)
-        nc.vector.memset(staged[:, 2 * R : 3 * R].bitcast(I32), 0)
-        nc.vector.memset(table[:], 0.0)
         nc.vector.memset(planes[:].bitcast(I32), 0)
         nc.vector.memset(g_plane[:, filler].bitcast(I32), 0)
         nc.vector.memset(g_codes[:, filler], 0)
@@ -143,18 +139,6 @@ def tile_mix_gradient_shared_by_neighbours_kernel(
         nc.sync.dma_start(out=wu_codes[:], in_=wu_words[0].rearrange("p n t -> p (n t)").bitcast(I32))
         load_scales((nc.sync,) * 4, wu_plane, wu_scales)
 
-        nc.scalar.activation(out=table[:, 4:5], in_=table[:, 0:1], func=ACT.Copy)
-
-        for rep in range(WARM_UP):
-            nc.tensor.matmul_mx(
-                out=banks[1][3][:],
-                lhsT=wd_raw[:, : 2 * P].bitcast(E2M1),
-                lhsT_scale=staged[:, 2 * R : 2 * R + P],
-                rhs=xq_codes[0][:].bitcast(E4M3),
-                rhs_scale=staged[:, 2 * R : 3 * R],
-                start=True,
-                stop=True,
-            )
 
         def cast_g(copy, h, cols):
             dst, src = cast_views(g_bf[h][:, cols, :], g_raw[h][:, :, cols])
@@ -303,16 +287,6 @@ def tile_mix_gradient_shared_by_neighbours_kernel(
             shared_part(nc.vector if j == PACK - 1 else nc.gpsimd, 1, j)
         first_layer(0)
         store(0)
-        for c in (2, 3, 3):
-            nc.tensor.matmul_mx(
-                out=banks[0][c][:],
-                lhsT=wu_codes[:, :P].bitcast(E4M3),
-                lhsT_scale=wu_plane[:, 0, :P],
-                rhs=dz_codes[:, :T].bitcast(E5M2),
-                rhs_scale=dz_plane[:, :T],
-                start=True,
-                stop=True,
-            )
         blend(2)
         blend(3)
         quantize_dz(2)

from contextlib import ExitStack

import concourse.mybir as mybir

N, L, R, K, T = 512, 1024, 512, 512, 512
FLOPS = 2 * R * T * (N + L) + 2 * K * T * R

F32 = mybir.dt.float32
BF16 = mybir.dt.bfloat16
I32 = mybir.dt.int32
U32 = mybir.dt.uint32
U16 = mybir.dt.uint16
U8 = mybir.dt.uint8
E4M3 = mybir.dt.float8_e4m3fn_x4
E5M2 = mybir.dt.float8_e5m2_x4
E2M1 = mybir.dt.float4_e2m1fn_x4
ALU = mybir.AluOpType
ACT = mybir.ActivationFunctionType
AXIS = mybir.AxisListType

P = 128
PACK = 4
GROUP = 4
HALF = T // 2
QUARTER = T // 4
G_DVE_COLS = 176
G_DVE_COLS_2 = 144


def load_scales(queues, plane, scales):
    rows = scales.bitcast(I32)
    for q, queue in enumerate(queues):
        queue.dma_start(
            out=plane[32 * q : 32 * q + 4, :, :].bitcast(I32),
            in_=rows[:, 4 * q : 4 * q + 4, :].rearrange("z r c -> r z c"),
        )


def regroup_words(nc, dst, src):
    nc.vector.tensor_copy(
        out=dst.bitcast(U16).rearrange("p (j a m) -> p a j m", j=PACK, m=8),
        in_=src.bitcast(U16).rearrange("p (a m j) -> p a j m", j=PACK, m=8),
    )


def regroup_scales(nc, dst, src):
    nc.vector.tensor_copy(
        out=dst.rearrange("p (j a m) -> p a j m", j=PACK, m=16),
        in_=src.rearrange("p (a m j) -> p a j m", j=PACK, m=16),
    )


def cast_views(dst, src):
    return (
        dst.rearrange("p (c i) j -> p c j i", i=4),
        src.rearrange("p j (c i) -> p c j i", i=4),
    )


def tile_mix_gradient_shared_by_neighbours_kernel(
    tc, g, wd_words, wd_scales, xq_words, xq_scales, ws_words, ws_scales, us, wu_words, wu_scales, out
):
    nc = tc.nc
    with ExitStack() as ctx:
        sb = ctx.enter_context(tc.tile_pool(name="sb", bufs=1))
        psum = ctx.enter_context(tc.psum_pool(name="psum", bufs=1))
        ctx.enter_context(tc.manual_schedule())

        def tile(name, shape, dtype):
            return sb.tile(shape, dtype, name=name, align_bytes=64)

        ws_raw = tile("ws_raw", [P, 4 * R], U8)
        wd_raw = tile("wd_raw", [P, 2 * R], U8)
        staged = tile("staged", [P, 4 * R], U8)
        planes = tile("planes", [P, 4 * R], U8)
        wd_plane_raw = tile("wd_plane_raw", [P, 1, R], U8)
        ws_codes = tile("ws_codes", [P, 4 * R], U8)
        ws_plane = tile("ws_plane", [P, 2 * R], U8)
        wd_codes = tile("wd_codes", [P, 2 * R], U8)
        wd_plane = tile("wd_plane", [P, R], U8)
        xq_codes = [tile("xq_codes%d" % h, [P, 2 * HALF], I32) for h in range(2)]
        wu_codes = tile("wu_codes", [P, K], I32)
        wu_plane = tile("wu_plane", [P, 1, K], U8)
        g_raw = [tile("g_raw%d" % h, [P, PACK, HALF], F32) for h in range(2)]
        g_bf = [tile("g_bf%d" % h, [P, HALF, PACK], BF16) for h in range(2)]
        g_codes = tile("g_codes", [P, 3 * HALF], U32)
        g_plane = tile("g_plane", [P, 3 * HALF], U8)
        us_sb = tile("us_sb", [P, PACK], F32)
        us_half = tile("us_half", [P, PACK], F32)
        us_eighth = tile("us_eighth", [P, PACK], F32)
        own = [tile("own%d" % h, [P, PACK, HALF], F32) for h in range(2)]
        sums = [tile("sums%d" % h, [P, PACK, HALF // GROUP], F32) for h in range(2)]
        shared = [tile("shared%d" % h, [P, PACK, HALF // GROUP], F32) for h in range(2)]
        dz_bf = [tile("dz_bf%d" % u, [P, QUARTER, PACK], BF16) for u in range(4)]
        dz_codes = tile("dz_codes", [P, 3 * HALF], U32)
        dz_plane = tile("dz_plane", [P, 3 * HALF], U8)
        res = [[tile("res%d_%d" % (h, c), [P, HALF], F32) for c in range(4)] for h in range(2)]
        banks = [[psum.tile([P, T], F32, name="bank%d_%d" % (h, j)) for j in range(PACK)] for h in range(2)]

        filler = slice(HALF, 2 * HALF)
        nc.gpsimd.memset(wd_plane_raw[:].bitcast(I32), 0)
        nc.vector.memset(planes[:].bitcast(I32), 0)
        nc.vector.memset(g_plane[:, filler].bitcast(I32), 0)
        nc.vector.memset(g_codes[:, filler], 0)
        nc.vector.memset(dz_plane[:, filler].bitcast(I32), 0)
        nc.vector.memset(dz_codes[:, filler], 0)
        nc.vector.memset(wu_plane[:].bitcast(I32), 0)

        staged_words = staged[:].bitcast(I32)
        plane_words = planes[:].bitcast(I32)
        row = R // 4

        def stage_scales(first, scales):
            nc.sync.dma_start(
                out=staged_words[0:16, first * row : (first + 2) * row].rearrange("q (z c) -> q z c", z=2),
                in_=scales.bitcast(I32).rearrange("z q c -> q z c"),
            )

        g_rows = g.rearrange("(p j) t -> p j t", j=PACK)
        xq_rows = xq_words.rearrange("z p n t -> p z (n t)").bitcast(I32)

        def load_xq(h):
            nc.sync.dma_start(
                out=xq_codes[h][:].rearrange("p (z t) -> p z t", z=2), in_=xq_rows[:, :, h * HALF : (h + 1) * HALF]
            )

        stage_scales(0, ws_scales)
        nc.sync.dma_start(out=wd_raw[:].bitcast(I32), in_=wd_words[0].bitcast(I32))
        stage_scales(2, xq_scales)
        load_scales((nc.scalar, nc.scalar, nc.scalar, nc.gpsimd), wd_plane_raw, wd_scales)
        nc.gpsimd.dma_start(out=us_sb[:], in_=us.rearrange("(p j) o -> p (j o)", j=PACK))
        load_xq(0)
        nc.sync.dma_start(out=g_raw[0][:], in_=g_rows[:, :, :HALF])
        for q in range(4):
            nc.sync.dma_start(out=plane_words[32 * q : 32 * q + 4, :], in_=staged_words[4 * q : 4 * q + 4, :])
        nc.sync.dma_start(out=ws_raw[:].bitcast(I32).rearrange("p (z c) -> p z c", z=2), in_=ws_words.bitcast(I32).rearrange("z p c -> p z c"))
        nc.sync.dma_start(out=g_raw[1][:], in_=g_rows[:, :, HALF:])
        load_xq(1)
        nc.sync.dma_start(out=wu_codes[:], in_=wu_words[0].rearrange("p n t -> p (n t)").bitcast(I32))
        load_scales((nc.sync,) * 4, wu_plane, wu_scales)


        def cast_g(copy, h, cols):
            dst, src = cast_views(g_bf[h][:, cols, :], g_raw[h][:, :, cols])
            copy(out=dst, in_=src)

        def quantize_g(h):
            cols = slice(2 * h * HALF, (2 * h + 1) * HALF)
            nc.vector.quantize_mx(
                out=g_codes[:, cols].bitcast(E5M2),
                scales=g_plane[:, cols],
                in_=g_bf[h][:].rearrange("p t j -> p (t j)"),
            )

        def first_sum_pass(h, j, w_codes, w_plane, at, cols, codes, plane, start, stop):
            nc.tensor.matmul_mx(
                out=banks[h][j][:, cols],
                lhsT=w_codes[:, 2 * P * at : 2 * P * (at + 1)].bitcast(E2M1),
                lhsT_scale=w_plane[:, P * at : P * (at + 1)],
                rhs=codes,
                rhs_scale=plane,
                start=start,
                stop=stop,
            )

        def first_sum(h):
            window = slice(h * HALF, h * HALF + T)
            for j in range(PACK):
                first_sum_pass(
                    h, j, wd_codes, wd_plane, j, slice(0, T), g_codes[:, window].bitcast(E5M2), g_plane[:, window], True, False
                )
            for j in range(PACK):
                for z in range(2):
                    for part in range(2):
                        first = h * HALF + part * QUARTER
                        at = z * HALF + part * QUARTER
                        first_sum_pass(
                            h,
                            j,
                            ws_codes,
                            ws_plane,
                            2 * j + z,
                            slice(first, first + QUARTER),
                            xq_codes[h][:, at : at + QUARTER].bitcast(E4M3),
                            planes[:, (2 + z) * R + first : (2 + z) * R + first + QUARTER],
                            False,
                            z == 1 and part == 1,
                        )

        def group_sums(h, j):
            nc.vector.tensor_reduce(
                out=sums[h][:, j, :],
                in_=banks[h][j][:, h * HALF : (h + 1) * HALF].rearrange("p (b i) -> p b i", i=GROUP),
                axis=AXIS.X,
                op=ALU.add,
            )

        def own_part(h, j):
            nc.scalar.activation(
                out=own[h][:, j, :],
                in_=banks[h][j][:, h * HALF : (h + 1) * HALF],
                func=ACT.Copy,
                scale=us_half[:, j : j + 1],
            )

        def shared_part(engine, h, j):
            engine.tensor_scalar(
                out=shared[h][:, j, :],
                in0=sums[h][:, j, :],
                scalar1=us_eighth[:, j : j + 1],
                scalar2=0.0,
                op0=ALU.mult,
                op1=ALU.add,
            )

        def blend(u):
            h, part = divmod(u, 2)
            groups = QUARTER // GROUP
            nc.vector.tensor_tensor(
                out=dz_bf[u][:].rearrange("p (b i) j -> p b j i", i=GROUP),
                in0=own[h][:, :, part * QUARTER : (part + 1) * QUARTER].rearrange("p j (b i) -> p b j i", i=GROUP),
                in1=shared[h][:, :, part * groups : (part + 1) * groups]
                .rearrange("p j b -> p b j")
                .unsqueeze(3)
                .to_broadcast([P, groups, PACK, GROUP]),
                op=ALU.add,
            )

        def quantize_dz(u):
            first = u * QUARTER + (u // 2) * HALF
            cols = slice(first, first + QUARTER)
            nc.vector.quantize_mx(
                out=dz_codes[:, cols].bitcast(E5M2),
                scales=dz_plane[:, cols],
                in_=dz_bf[u][:].rearrange("p t j -> p (t j)"),
            )

        def first_layer(h):
            window = slice(h * HALF, h * HALF + T)
            for c in range(4):
                nc.tensor.matmul_mx(
                    out=banks[h][c][:],
                    lhsT=wu_codes[:, P * c : P * (c + 1)].bitcast(E4M3),
                    lhsT_scale=wu_plane[:, 0, P * c : P * (c + 1)],
                    rhs=dz_codes[:, window].bitcast(E5M2),
                    rhs_scale=dz_plane[:, window],
                    start=True,
                    stop=True,
                )

        def store(h):
            tokens = slice(h * HALF, (h + 1) * HALF)
            for c in range(4):
                if h == 1 and c % 2 == 1:
                    nc.vector.tensor_copy(out=res[h][c][:], in_=banks[h][c][:, tokens])
                else:
                    nc.scalar.copy(out=res[h][c][:], in_=banks[h][c][:, tokens])
                nc.sync.dma_start(out=out[P * c : P * (c + 1), tokens], in_=res[h][c][:])

        regroup_words(nc, wd_codes[:], wd_raw[:])
        cast_g(nc.vector.tensor_copy, 0, slice(0, G_DVE_COLS))
        cast_g(nc.scalar.copy, 0, slice(G_DVE_COLS, HALF))
        nc.scalar.activation(out=us_half[:], in_=us_sb[:], func=ACT.Copy, scale=0.5)
        nc.scalar.activation(out=us_eighth[:], in_=us_sb[:], func=ACT.Copy, scale=0.5 / GROUP)
        regroup_scales(nc, wd_plane[:], wd_plane_raw[:, 0, :])
        quantize_g(0)
        regroup_scales(nc, ws_plane[:], planes[:, : 2 * R])
        regroup_words(nc, ws_codes[:], ws_raw[:])
        first_sum(0)
        cast_g(nc.vector.tensor_copy, 1, slice(0, G_DVE_COLS_2))
        cast_g(nc.scalar.copy, 1, slice(G_DVE_COLS_2, HALF))
        quantize_g(1)
        first_sum(1)
        for js, jo in ((0, 1), (2, 0), (3, 2), (1, 3)):
            group_sums(0, js)
            own_part(0, jo)
            shared_part(nc.vector if js == 1 else nc.gpsimd, 0, js)
        for j in range(PACK):
            own_part(1, j)
        blend(0)
        blend(1)
        quantize_dz(0)
        for j in range(PACK):
            group_sums(1, j)
            if j == 0:
                quantize_dz(1)
            shared_part(nc.vector if j == PACK - 1 else nc.gpsimd, 1, j)
        first_layer(0)
        store(0)
        blend(2)
        blend(3)
        quantize_dz(2)
        quantize_dz(3)
        first_layer(1)
        store(1)
